import numpy as np
import ml_dtypes


def mxq(x, axis, fmt="e4m3"):
    dtype, down = {"e4m3": (ml_dtypes.float8_e4m3fn, 7), "e5m2": (ml_dtypes.float8_e5m2, 14)}[fmt]
    v = np.moveaxis(np.asarray(x, np.float32).astype(ml_dtypes.bfloat16).astype(np.float64), axis, -1)
    blocks = v.reshape(v.shape[:-1] + (-1, 32))
    amax = np.abs(blocks).max(-1, keepdims=True)
    byte = np.maximum(np.where(amax > 0, np.frexp(amax)[1] - 1 + 127, 0) - down, 1)
    scale = np.exp2(byte - 127.0)
    codes = (blocks / scale).astype(np.float32).astype(dtype).astype(np.float64)
    return np.moveaxis((codes * scale).reshape(v.shape), -1, axis)


WIDE = False


def mx_kscale(k):
    if not WIDE:
        return np.ones(k)
    levels = np.array([10, -10, 5, -5, 0])
    if k % 512:
        return np.exp2(np.random.permutation(np.resize(levels, k // 32))).repeat(32)
    a = np.empty((k // 512, 16))
    for p in range(k // 512):
        a[p, :8] = np.random.permutation(np.resize(levels, 8))
        for g in range(8):
            far = levels[np.abs(levels - a[p, g]) >= 10]
            a[p, g + 8] = far[np.random.randint(len(far))]
    return np.exp2(a.ravel()).repeat(32)


def f64(x):
    return np.asarray(x).astype(np.float64)


def striped8(idx):
    return np.concatenate([x.reshape(-1, 16).T for x in idx]).astype(np.uint16)


def runs(offs, k):
    lists = np.stack([offs[16 * r : 16 * r + 16].T.reshape(-1) for r in range(8)]).astype(np.int64)
    return lists[np.arange(k) % 512 // 64]


def pack_weight(w):
    k, n = w.shape
    w = f64(np.asarray(w, np.float32).astype(ml_dtypes.bfloat16)).reshape(k // 32, 32, n)
    amax = np.abs(w).max(1)
    byte = np.clip(np.where(amax > 0, np.frexp(amax)[1] - 1 + 127 - 7, 1), 1, 254)
    scaled = (w * np.exp2(127.0 - byte)[:, None, :]).reshape(k, n).astype(np.float32)
    words = np.ascontiguousarray(scaled.reshape(k // 512, 128, 4, n).transpose(0, 1, 3, 2)).astype(ml_dtypes.float8_e4m3fn).view(np.uint8)
    return words, np.ascontiguousarray(byte.astype(np.uint8).reshape(k // 512, 16, n))


def unpack_weight(words, scales):
    g, p, n, _ = words.shape
    vals = np.ascontiguousarray(words).view(ml_dtypes.float8_e4m3fn).astype(np.float64) * np.repeat(np.exp2(scales.astype(np.float64) - 127.0), 8, axis=1)[..., None]
    return vals.transpose(0, 1, 3, 2).reshape(g * 512, n)


E2M1 = np.array([0.0, 0.5, 1.0, 1.5, 2.0, 3.0, 4.0, 6.0, -0.0, -0.5, -1.0, -1.5, -2.0, -3.0, -4.0, -6.0])


def pack_fp4(w):
    k, n = w.shape
    w = f64(np.asarray(w, np.float32).astype(ml_dtypes.bfloat16)).reshape(k // 32, 32, n)
    amax = np.abs(w).max(1)
    mant, ex = np.frexp(amax / 6.0)
    byte = np.clip(np.where(amax > 0, np.where(mant > 0.5, ex, ex - 1) + 127, 1), 1, 254)
    scaled = (w * np.exp2(127.0 - byte)[:, None, :]).reshape(k, n).astype(np.float32)
    c = np.ascontiguousarray(scaled.reshape(k // 512, 128, 4, n).transpose(0, 1, 3, 2)).astype(ml_dtypes.float4_e2m1fn).view(np.uint8) & 0xF
    words = (c[..., 0::2] | (c[..., 1::2] << 4)).reshape(k // 512, 128, 2 * n)
    return np.ascontiguousarray(words), np.ascontiguousarray(byte.astype(np.uint8).reshape(k // 512, 16, n))


def unpack_fp4(words, scales):
    g, _, n = scales.shape
    words = np.ascontiguousarray(words).reshape(g, 128, n, 2)
    nib = np.empty((g, 128, n, 4), np.uint8)
    nib[..., 0::2] = words & 0xF
    nib[..., 1::2] = words >> 4
    vals = E2M1[nib] * np.repeat(np.exp2(scales.astype(np.float64) - 127.0), 8, axis=1)[..., None]
    return vals.transpose(0, 1, 3, 2).reshape(g * 512, n)


K, T, S, H, G, U = 512, 2048, 512, 512, 2048, 1024


def setup_inputs():
    n = np.random.standard_normal
    s = mx_kscale(K)[:, None]
    packed_xT = pack_weight(n((K, T)) * s)
    packed_w1 = pack_fp4(n((K, H)) / np.sqrt(K) / s)
    packed_dT = pack_weight(n((K, G)) / s)
    perm = np.stack([np.random.permutation(U) for _ in range(8)])
    return {
        "x_words": packed_xT[0],
        "x_scales": packed_xT[1],
        "w1_words": packed_w1[0],
        "w1_scales": packed_w1[1],
        "gs": (np.random.uniform(0.5, 1.5, (K, 1)) * s).astype(np.float32),
        "d_words": packed_dT[0],
        "d_scales": packed_dT[1],
        "offs": striped8(np.random.randint(0, T, (8, S))),
        "n1": striped8(np.stack([np.random.permutation(S) for _ in range(8)])),
        "n2": striped8(np.stack([np.random.permutation(S) for _ in range(8)])),
        "k1": striped8(np.random.randint(0, G, (8, H))),
        "n3": striped8(perm[:, :S]),
        "n4": striped8(perm[:, S:]),
        "n5": striped8(np.stack([np.random.permutation(S) for _ in range(8)])),
    }


def reference(x_words, x_scales, w1_words, w1_scales, gs, d_words, d_scales, offs, n1, n2, k1, n3, n4, n5):
    d_k1 = unpack_weight(d_words, d_scales)[np.arange(K)[:, None], runs(k1, K)]
    xq = unpack_weight(x_words, x_scales)[np.arange(K)[:, None], runs(offs, K)]
    y = unpack_fp4(w1_words, w1_scales).T @ xq
    z = f64(gs) * (y - (np.minimum(y[np.arange(H)[:, None], runs(n1, H)], y[np.arange(H)[:, None], runs(n2, H)])))
    h = 0.0625 * ((d_k1.T @ mxq(z, 0, "e4m3")))
    dn = np.minimum(h, h[np.arange(H)[:, None], runs(n5, H)])
    up = np.maximum(h, h[np.arange(H)[:, None], runs(n5, H)])
    ph = np.zeros((H, U))
    ph[np.arange(H)[:, None], runs(n3, H)] = up
    out = ph.copy()
    out[np.arange(H)[:, None], runs(n4, H)] = dn
    return out

@@ -1,0 +1,195 @@
+from contextlib import ExitStack
+
+import concourse.mybir as mybir
+
+F32 = mybir.dt.float32
+BF16 = mybir.dt.bfloat16
+I32 = mybir.dt.int32
+U32 = mybir.dt.uint32
+U16 = mybir.dt.uint16
+U8 = mybir.dt.uint8
+FP8X4 = mybir.dt.float8_e4m3fn_x4
+FP4X4 = mybir.dt.float4_e2m1fn_x4
+ALU = mybir.AluOpType
+ACT = mybir.ActivationFunctionType
+
+P = 128
+PACK = 4
+TABLE = 2048
+S = 512
+PAGE = 1024
+HALF = 256
+FLOPS = 2 * 2 * 512 * 512 * 512
+
+
+def tile_picked_hdenseunderpagmx_none_p_kernel(
+    tc, x_words, x_scales, w1_words, w1_scales, gs, d_words, d_scales, offs, n1, n2, k1, n3, n4, n5, out
+):
+    nc = tc.nc
+    with ExitStack() as ctx:
+        keep = ctx.enter_context(tc.tile_pool(name="keep", bufs=1))
+        psum = ctx.enter_context(tc.psum_pool(name="psum", bufs=1))
+
+        def load_list(name, src):
+            tile = keep.tile([P, S // 16], U16, name=name)
+            nc.sync.dma_start(tile[:], src)
+            return tile
+
+        def entries(lst, c):
+            return lst[:, c * HALF // 16 : (c + 1) * HALF // 16]
+
+        def cols(c):
+            return slice(c * HALF, (c + 1) * HALF)
+
+        xs_win = keep.tile([P, TABLE], U8, name="xs_win", align_bytes=64)
+        nc.sync.dma_start(
+            xs_win[:].bitcast(I32), x_scales[0].bitcast(I32).unsqueeze(1).to_broadcast([16, 8, TABLE // 4])
+        )
+        offs_t = load_list("offs_t", offs)
+        xw_win = keep.tile([P, TABLE], I32, name="xw_win", tag="table", align_bytes=64)
+        nc.sync.dma_start(xw_win[:], x_words[0].rearrange("p n t -> p (n t)").bitcast(I32))
+        ws_raw = keep.tile([P, S], U8, name="ws_raw", align_bytes=64)
+        ws_rows = w1_scales[0].bitcast(I32).rearrange("(q r) n -> r q n", r=4)
+        for r in range(4):
+            nc.scalar.dma_start(
+                ws_raw[r:P:4, :].bitcast(I32), ws_rows[r].unsqueeze(1).to_broadcast([4, 8, S // 4])
+            )
+        k1_t = load_list("k1_t", k1)
+        n1_t = load_list("n1_t", n1)
+        n2_t = load_list("n2_t", n2)
+        n5_t = load_list("n5_t", n5)
+        n3_t = load_list("n3_t", n3)
+        n4_t = load_list("n4_t", n4)
+
+        w_raw = keep.tile([P, 2 * S], U8, name="w_raw", align_bytes=64)
+        nc.gpsimd.dma_start(w_raw[:].bitcast(I32), w1_words[0].bitcast(I32))
+        ds_win = keep.tile([P, TABLE], U8, name="ds_win", align_bytes=64)
+        nc.gpsimd.memset(ds_win[:].bitcast(I32), 0)
+        nc.gpsimd.dma_start(ds_win[0:P:8, :].bitcast(I32), d_scales[0].bitcast(I32))
+        gs_t = keep.tile([P, PACK], F32, name="gs_t")
+        nc.gpsimd.dma_start(gs_t[:], gs.rearrange("(p t) o -> p (t o)", t=PACK))
+
+        xs_got = keep.tile([P, S], U8, name="xs_got", align_bytes=64)
+        nc.vector.tensor_copy(xs_got[:], xs_win[:].indirect(offs_t[:]))
+        xs = keep.tile([P, S], U8, name="xs", align_bytes=64)
+        nc.vector.tensor_copy(xs[:].bitcast(I32), xs_got[:].bitcast(I32))
+        for r in range(1, 4):
+            nc.scalar.dma_start(xs[r:P:32, :].bitcast(I32), xs_got[8 * r : P : 32, :].bitcast(I32))
+
+        w = keep.tile([P, 2 * S], U8, name="w", align_bytes=64)
+        nc.scalar.copy(
+            w[:].bitcast(U16).rearrange("p (t m) -> p t m", t=PACK),
+            w_raw[:].bitcast(U16).rearrange("p (m t) -> p t m", t=PACK),
+        )
+        ws = keep.tile([P, S], U8, name="ws", align_bytes=64)
+        nc.vector.tensor_copy(
+            ws[:].rearrange("p (t m) -> p t m", t=PACK), ws_raw[:].rearrange("p (m t) -> p t m", t=PACK)
+        )
+
+        xw = keep.tile([P, S], U32, name="xw", align_bytes=64)
+        y = [keep.tile([P, S], F32, name="y%d" % t) for t in range(PACK)]
+        for c in range(2):
+            nc.vector.tensor_copy(xw[:, cols(c)], xw_win[:].bitcast(U32).indirect(entries(offs_t, c)))
+        for t in range(PACK):
+            for c in range(2):
+                y_ps = psum.tile([P, HALF], F32, name="y_ps", tag="bank%d%d" % (t, c))
+                nc.tensor.matmul_mx(
+                    out=y_ps[:],
+                    lhsT=w[:, 2 * P * t : 2 * P * (t + 1)].bitcast(FP4X4),
+                    lhsT_scale=ws[:, P * t : P * (t + 1)],
+                    rhs=xw[:, cols(c)].bitcast(FP8X4),
+                    rhs_scale=xs[:, cols(c)],
+                    start=True,
+                    stop=True,
+                )
+                if c == 0:
+                    nc.scalar.copy(y[t][:, cols(c)], y_ps[:])
+                else:
+                    nc.vector.tensor_copy(y[t][:, cols(c)], y_ps[:])
+
+        dw_win = keep.tile([P, TABLE], I32, name="dw_win", tag="table", align_bytes=64)
+        nc.sync.dma_start(dw_win[:], d_words[0].rearrange("p n t -> p (n t)").bitcast(I32))
+
+        ds_got = keep.tile([P, S], U8, name="ds_got", align_bytes=64)
+        nc.vector.tensor_copy(ds_got[:], ds_win[:].indirect(k1_t[:]))
+        ds = keep.tile([P, S], U8, name="ds", align_bytes=64)
+        nc.vector.tensor_copy(
+            ds[:].rearrange("p (t m) -> p t m", t=PACK), ds_got[:].rearrange("p (m t) -> p t m", t=PACK)
+        )
+        for r in range(1, 4):
+            nc.sync.dma_start(ds[r:P:32, :].bitcast(I32), ds[8 * r : P : 32, :].bitcast(I32))
+
+        zw = keep.tile([P, S], U32, name="zw", align_bytes=64)
+        zs = keep.tile([P, S], U8, name="zs", align_bytes=64)
+        dw_got = keep.tile([P, S], U32, name="dw_got", align_bytes=64)
+        dw = keep.tile([P, S], U32, name="dw", align_bytes=64)
+        h_ps = {}
+        h = [keep.tile([P, S], F32, name="h%d" % t) for t in range(PACK)]
+        for c in range(2):
+            zp = keep.tile([P, PACK, HALF], BF16, name="zp%d" % c, align_bytes=64)
+            for t in range(PACK):
+                g1 = keep.tile([P, HALF], F32, name="g1", bufs=4)
+                g2 = keep.tile([P, HALF], F32, name="g2", bufs=4)
+                nc.scalar.activation(g1[:], y[t][:].indirect(entries(n1_t, c)), ACT.Copy)
+                if c == 0 and t < 2:
+                    nc.vector.tensor_copy(g2[:], y[t][:].indirect(entries(n2_t, c)))
+                else:
+                    nc.scalar.activation(g2[:], y[t][:].indirect(entries(n2_t, c)), ACT.Copy)
+                low = keep.tile([P, HALF], F32, name="low", bufs=2)
+                nc.vector.tensor_tensor(low[:], g1[:], g2[:], ALU.min)
+                diff = keep.tile([P, HALF], F32, name="diff", bufs=2)
+                nc.vector.tensor_tensor(diff[:], y[t][:, cols(c)], low[:], ALU.subtract)
+                nc.vector.tensor_scalar(zp[:, t, :], diff[:], gs_t[:, t : t + 1], None, ALU.mult)
+            zi = keep.tile([P, HALF, PACK], BF16, name="zi%d" % c, align_bytes=64)
+            nc.vector.tensor_copy(
+                zi[:].rearrange("p (a i) t -> p a t i", i=4), zp[:].rearrange("p t (a i) -> p a t i", i=4)
+            )
+            nc.vector.quantize_mx(
+                out=zw[:, cols(c)].bitcast(FP8X4), scales=zs[:, cols(c)], in_=zi[:].rearrange("p n t -> p (n t)")
+            )
+            if c == 0:
+                nc.vector.tensor_copy(dw_got[:], dw_win[:].bitcast(U32).indirect(k1_t[:]))
+                nc.vector.tensor_copy(
+                    dw[:].rearrange("p (t m) -> p m t", t=PACK), dw_got[:].rearrange("p (m t) -> p m t", t=PACK)
+                )
+            for t in range(PACK):
+                h_ps[t, c] = psum.tile([P, HALF], F32, name="h_ps", tag="bank%d%d" % (t, c))
+                nc.tensor.matmul_mx(
+                    out=h_ps[t, c][:],
+                    lhsT=dw[:, P * t : P * (t + 1)].bitcast(FP8X4),
+                    lhsT_scale=ds[:, P * t : P * (t + 1)],
+                    rhs=zw[:, cols(c)].bitcast(FP8X4),
+                    rhs_scale=zs[:, cols(c)],
+                    start=True,
+                    stop=True,
+                )
+
+        out_rows = out.rearrange("(p t) w -> t p w", t=PACK)
+        for t in range(PACK):
+            nc.scalar.activation(h[t][:, cols(0)], h_ps[t, 0][:], ACT.Copy, scale=0.0625)
+            if t == 0:
+                nc.vector.tensor_scalar(h[t][:, cols(1)], h_ps[t, 1][:], 0.0625, None, ALU.mult)
+            else:
+                nc.scalar.activation(h[t][:, cols(1)], h_ps[t, 1][:], ACT.Copy, scale=0.0625)
+            g5 = keep.tile([P, S], F32, name="g5_%d" % t)
+            for c in range(2):
+                nc.scalar.activation(g5[:, cols(c)], h[t][:].indirect(entries(n5_t, c)), ACT.Copy)
+            page = keep.tile([P, PAGE], F32, name="page%d" % t)
+            if t == 0:
+                up = keep.tile([P, S], F32, name="up%d" % t)
+                dn = keep.tile([P, S], F32, name="dn%d" % t)
+                for c in range(2):
+                    nc.vector.tensor_tensor(up[:, cols(c)], h[t][:, cols(c)], g5[:, cols(c)], ALU.max)
+                    nc.vector.tensor_copy(page[:].indirect(entries(n3_t, c)), up[:, cols(c)])
+                nc.vector.tensor_tensor(dn[:], h[t][:], g5[:], ALU.min)
+                nc.vector.tensor_copy(page[:].indirect(n4_t[:]), dn[:])
+            else:
+                gap = keep.tile([P, S], F32, name="gap%d" % t)
+                nc.vector.tensor_tensor(gap[:], g5[:], h[t][:], ALU.subtract)
+                rise = keep.tile([P, S], F32, name="rise%d" % t)
+                fall = keep.tile([P, S], F32, name="fall%d" % t)
+                nc.scalar.activation(rise[:], gap[:], ACT.Relu)
+                nc.scalar.activation(fall[:], rise[:], ACT.Copy, scale=-1.0)
+                nc.vector.tensor_tensor(page[:].indirect(n3_t[:]), h[t][:], rise[:], ALU.add)
+                nc.vector.tensor_tensor(page[:].indirect(n4_t[:]), g5[:], fall[:], ALU.add)
+            nc.sync.dma_start(out_rows[t], page[:])

@@ -41,21 +41,19 @@ def tile_picked_hdenseunderpagmx_none_p_kernel(
         def cols(c):
             return slice(c * HALF, (c + 1) * HALF)
 
-        xs_win = keep.tile([P, TABLE], U8, name="xs_win", align_bytes=64)
-        nc.sync.dma_start(
-            xs_win[:].bitcast(I32), x_scales[0].bitcast(I32).unsqueeze(1).to_broadcast([16, 8, TABLE // 4])
-        )
-        offs_t = load_list("offs_t", offs)
-        xw_win = keep.tile([P, TABLE], I32, name="xw_win", tag="table", align_bytes=64)
-        nc.sync.dma_start(xw_win[:], x_words[0].rearrange("p n t -> p (n t)").bitcast(I32))
+        def spread(scales):
+            rows = scales[0].bitcast(I32)
+            return rows.unsqueeze(1).to_broadcast([16, 8, rows.shape[1]])
+
         ws_raw = keep.tile([P, S], U8, name="ws_raw", align_bytes=64)
-        ws_rows = w1_scales[0].bitcast(I32).rearrange("(q r) n -> r q n", r=4)
-        for r in range(4):
-            nc.scalar.dma_start(
-                ws_raw[r:P:4, :].bitcast(I32), ws_rows[r].unsqueeze(1).to_broadcast([4, 8, S // 4])
-            )
+        nc.sync.dma_start(ws_raw[:].bitcast(I32), spread(w1_scales))
+        xs_win = keep.tile([P, TABLE], U8, name="xs_win", align_bytes=64)
+        nc.sync.dma_start(xs_win[:].bitcast(I32), spread(x_scales))
+        offs_t = load_list("offs_t", offs)
         k1_t = load_list("k1_t", k1)
         n1_t = load_list("n1_t", n1)
+        xw_win = keep.tile([P, TABLE], I32, name="xw_win", tag="table", align_bytes=64)
+        nc.sync.dma_start(xw_win[:], x_words[0].rearrange("p n t -> p (n t)").bitcast(I32))
         n2_t = load_list("n2_t", n2)
         n5_t = load_list("n5_t", n5)
         n3_t = load_list("n3_t", n3)
@@ -64,49 +62,37 @@ def tile_picked_hdenseunderpagmx_none_p_kernel(
         w_raw = keep.tile([P, 2 * S], U8, name="w_raw", align_bytes=64)
         nc.gpsimd.dma_start(w_raw[:].bitcast(I32), w1_words[0].bitcast(I32))
         ds_win = keep.tile([P, TABLE], U8, name="ds_win", align_bytes=64)
-        nc.gpsimd.memset(ds_win[:].bitcast(I32), 0)
+        nc.vector.memset(ds_win[:].bitcast(I32), 0)
         nc.gpsimd.dma_start(ds_win[0:P:8, :].bitcast(I32), d_scales[0].bitcast(I32))
         gs_t = keep.tile([P, PACK], F32, name="gs_t")
         nc.gpsimd.dma_start(gs_t[:], gs.rearrange("(p t) o -> p (t o)", t=PACK))
 
+        planes = keep.tile([P, 2 * S], U8, name="planes", align_bytes=64)
+        xs = planes[:, 0:S]
+        ws = planes[:, S : 2 * S]
+        staged = keep.tile([P, 2 * S], U8, name="staged", align_bytes=64)
         xs_got = keep.tile([P, S], U8, name="xs_got", align_bytes=64)
+        nc.vector.tensor_copy(
+            staged[:, S : 2 * S].rearrange("p (t m) -> p t m", t=PACK), ws_raw[:].rearrange("p (m t) -> p t m", t=PACK)
+        )
         nc.vector.tensor_copy(xs_got[:], xs_win[:].indirect(offs_t[:]))
-        xs = keep.tile([P, S], U8, name="xs", align_bytes=64)
-        nc.vector.tensor_copy(xs[:].bitcast(I32), xs_got[:].bitcast(I32))
+        nc.vector.tensor_copy(ws.bitcast(I32), staged[:, S : 2 * S].bitcast(I32))
+        nc.vector.tensor_copy(staged[:, 0:S].bitcast(I32), xs_got[:].bitcast(I32))
+        nc.vector.tensor_copy(xs.bitcast(I32), xs_got[:].bitcast(I32))
         for r in range(1, 4):
-            nc.scalar.dma_start(xs[r:P:32, :].bitcast(I32), xs_got[8 * r : P : 32, :].bitcast(I32))
+            nc.scalar.dma_start(planes[r:P:32, :].bitcast(I32), staged[8 * r : P : 32, :].bitcast(I32))
 
         w = keep.tile([P, 2 * S], U8, name="w", align_bytes=64)
         nc.scalar.copy(
             w[:].bitcast(U16).rearrange("p (t m) -> p t m", t=PACK),
             w_raw[:].bitcast(U16).rearrange("p (m t) -> p t m", t=PACK),
         )
-        ws = keep.tile([P, S], U8, name="ws", align_bytes=64)
-        nc.vector.tensor_copy(
-            ws[:].rearrange("p (t m) -> p t m", t=PACK), ws_raw[:].rearrange("p (m t) -> p t m", t=PACK)
-        )
 
         xw = keep.tile([P, S], U32, name="xw", align_bytes=64)
         y = [keep.tile([P, S], F32, name="y%d" % t) for t in range(PACK)]
+        y_ps = [[psum.tile([P, 2, HALF], F32, name="y_ps%d%d" % (c, a)) for a in range(2)] for c in range(2)]
         for c in range(2):
             nc.vector.tensor_copy(xw[:, cols(c)], xw_win[:].bitcast(U32).indirect(entries(offs_t, c)))
-        for t in range(PACK):
-            for c in range(2):
-                y_ps = psum.tile([P, HALF], F32, name="y_ps", tag="bank%d%d" % (t, c))
-                nc.tensor.matmul_mx(
-                    out=y_ps[:],
-                    lhsT=w[:, 2 * P * t : 2 * P * (t + 1)].bitcast(FP4X4),
-                    lhsT_scale=ws[:, P * t : P * (t + 1)],
-                    rhs=xw[:, cols(c)].bitcast(FP8X4),
-                    rhs_scale=xs[:, cols(c)],
-                    start=True,
-                    stop=True,
-                )
-                if c == 0:
-                    nc.scalar.copy(y[t][:, cols(c)], y_ps[:])
-                else:
-                    nc.vector.tensor_copy(y[t][:, cols(c)], y_ps[:])
-
         dw_win = keep.tile([P, TABLE], I32, name="dw_win", tag="table", align_bytes=64)
         nc.sync.dma_start(dw_win[:], d_words[0].rearrange("p n t -> p (n t)").bitcast(I32))
 
@@ -119,27 +105,51 @@ def tile_picked_hdenseunderpagmx_none_p_kernel(
         for r in range(1, 4):
             nc.sync.dma_start(ds[r:P:32, :].bitcast(I32), ds[8 * r : P : 32, :].bitcast(I32))
 
+        for a in range(2):
+            for c in range(2):
+                for t in (2 * a, 2 * a + 1):
+                    nc.tensor.matmul_mx(
+                        out=y_ps[c][a][:, t % 2, :],
+                        lhsT=w[:, 2 * P * t : 2 * P * (t + 1)].bitcast(FP4X4),
+                        lhsT_scale=ws[:, P * t : P * (t + 1)],
+                        rhs=xw[:, cols(c)].bitcast(FP8X4),
+                        rhs_scale=xs[:, cols(c)],
+                        start=True,
+                        stop=True,
+                    )
+                for t in (2 * a, 2 * a + 1):
+                    if c == 0:
+                        nc.scalar.copy(y[t][:, cols(c)], y_ps[c][a][:, t % 2, :])
+                    else:
+                        nc.vector.tensor_copy(y[t][:, cols(c)], y_ps[c][a][:, t % 2, :])
+
         zw = keep.tile([P, S], U32, name="zw", align_bytes=64)
         zs = keep.tile([P, S], U8, name="zs", align_bytes=64)
         dw_got = keep.tile([P, S], U32, name="dw_got", align_bytes=64)
         dw = keep.tile([P, S], U32, name="dw", align_bytes=64)
-        h_ps = {}
-        h = [keep.tile([P, S], F32, name="h%d" % t) for t in range(PACK)]
+        h_ps = [[psum.tile([P, 2, HALF], F32, name="h_ps%d%d" % (c, a)) for a in range(2)] for c in range(2)]
+        h = [keep.tile([P, S], F32, name="h", tag="h%d" % t) for t in range(PACK)]
         for c in range(2):
             zp = keep.tile([P, PACK, HALF], BF16, name="zp%d" % c, align_bytes=64)
-            for t in range(PACK):
-                g1 = keep.tile([P, HALF], F32, name="g1", bufs=4)
-                g2 = keep.tile([P, HALF], F32, name="g2", bufs=4)
-                nc.scalar.activation(g1[:], y[t][:].indirect(entries(n1_t, c)), ACT.Copy)
-                if c == 0 and t < 2:
-                    nc.vector.tensor_copy(g2[:], y[t][:].indirect(entries(n2_t, c)))
-                else:
-                    nc.scalar.activation(g2[:], y[t][:].indirect(entries(n2_t, c)), ACT.Copy)
-                low = keep.tile([P, HALF], F32, name="low", bufs=2)
-                nc.vector.tensor_tensor(low[:], g1[:], g2[:], ALU.min)
-                diff = keep.tile([P, HALF], F32, name="diff", bufs=2)
-                nc.vector.tensor_tensor(diff[:], y[t][:, cols(c)], low[:], ALU.subtract)
-                nc.vector.tensor_scalar(zp[:, t, :], diff[:], gs_t[:, t : t + 1], None, ALU.mult)
+            for a in range(2):
+                g1 = keep.tile([P, 2, HALF], F32, name="g1_%d%d" % (c, a))
+                g2 = keep.tile([P, 2, HALF], F32, name="g2_%d%d" % (c, a))
+                low = keep.tile([P, 2, HALF], F32, name="low%d%d" % (c, a))
+                diff = keep.tile([P, 2, HALF], F32, name="diff%d%d" % (c, a))
+                for j in range(2):
+                    t = 2 * a + j
+                    nc.scalar.activation(g1[:, j, :], y[t][:].indirect(entries(n1_t, c)), ACT.Copy)
+                    if c == 0 and a == 0:
+                        nc.vector.tensor_copy(g2[:, j, :], y[t][:].indirect(entries(n2_t, c)))
+                    else:
+                        nc.scalar.activation(g2[:, j, :], y[t][:].indirect(entries(n2_t, c)), ACT.Copy)
+                spans = [slice(0, 1), slice(1, 2)] if (c, a) == (1, 1) else [slice(0, 2)]
+                for span in spans:
+                    nc.vector.tensor_tensor(low[:, span, :], g1[:, span, :], g2[:, span, :], ALU.min)
+                    nc.vector.tensor_tensor(diff[:, span, :], y_ps[c][a][:, span, :], low[:, span, :], ALU.subtract)
+                    for j in range(span.start, span.stop):
+                        t = 2 * a + j
+                        nc.vector.tensor_scalar(zp[:, t, :], diff[:, j, :], gs_t[:, t : t + 1], None, ALU.mult)
             zi = keep.tile([P, HALF, PACK], BF16, name="zi%d" % c, align_bytes=64)
             nc.vector.tensor_copy(
                 zi[:].rearrange("p (a i) t -> p a t i", i=4), zp[:].rearrange("p t (a i) -> p a t i", i=4)
@@ -153,9 +163,8 @@ def tile_picked_hdenseunderpagmx_none_p_kernel(
                     dw[:].rearrange("p (t m) -> p m t", t=PACK), dw_got[:].rearrange("p (m t) -> p m t", t=PACK)
                 )
             for t in range(PACK):
-                h_ps[t, c] = psum.tile([P, HALF], F32, name="h_ps", tag="bank%d%d" % (t, c))
                 nc.tensor.matmul_mx(
-                    out=h_ps[t, c][:],
+                    out=h_ps[c][t // 2][:, t % 2, :],
                     lhsT=dw[:, P * t : P * (t + 1)].bitcast(FP8X4),
                     lhsT_scale=ds[:, P * t : P * (t + 1)],
                     rhs=zw[:, cols(c)].bitcast(FP8X4),
@@ -165,31 +174,51 @@ def tile_picked_hdenseunderpagmx_none_p_kernel(
                 )
 
         out_rows = out.rearrange("(p t) w -> t p w", t=PACK)
-        for t in range(PACK):
-            nc.scalar.activation(h[t][:, cols(0)], h_ps[t, 0][:], ACT.Copy, scale=0.0625)
+        g5 = {}
+        rise = {}
+        gap_tag = {1: "gap1", 2: "gap2", 3: "h1"}
+        g5_tag = ["g5_0", "g5_1", "g5_2", gap_tag[1]]
+        up = [keep.tile([P, S], F32, name="up%d" % t) for t in range(PACK)]
+        dn = [keep.tile([P, S], F32, name="dn%d" % t) for t in range(PACK)]
+        page = [keep.tile([P, PAGE], F32, name="page%d" % t) for t in range(PACK)]
+
+        def fetch(t):
+            nc.scalar.activation(h[t][:, cols(0)], h_ps[0][t // 2][:, t % 2, :], ACT.Copy, scale=0.0625)
             if t == 0:
-                nc.vector.tensor_scalar(h[t][:, cols(1)], h_ps[t, 1][:], 0.0625, None, ALU.mult)
+                nc.vector.tensor_scalar(h[t][:, cols(1)], h_ps[1][t // 2][:, t % 2, :], 0.0625, None, ALU.mult)
             else:
-                nc.scalar.activation(h[t][:, cols(1)], h_ps[t, 1][:], ACT.Copy, scale=0.0625)
-            g5 = keep.tile([P, S], F32, name="g5_%d" % t)
+                nc.scalar.activation(h[t][:, cols(1)], h_ps[1][t // 2][:, t % 2, :], ACT.Copy, scale=0.0625)
+            g5[t] = keep.tile([P, S], F32, name="g5", tag=g5_tag[t])
             for c in range(2):
-                nc.scalar.activation(g5[:, cols(c)], h[t][:].indirect(entries(n5_t, c)), ACT.Copy)
-            page = keep.tile([P, PAGE], F32, name="page%d" % t)
-            if t == 0:
-                up = keep.tile([P, S], F32, name="up%d" % t)
-                dn = keep.tile([P, S], F32, name="dn%d" % t)
-                for c in range(2):
-                    nc.vector.tensor_tensor(up[:, cols(c)], h[t][:, cols(c)], g5[:, cols(c)], ALU.max)
-                    nc.vector.tensor_copy(page[:].indirect(entries(n3_t, c)), up[:, cols(c)])
-                nc.vector.tensor_tensor(dn[:], h[t][:], g5[:], ALU.min)
-                nc.vector.tensor_copy(page[:].indirect(n4_t[:]), dn[:])
-            else:
-                gap = keep.tile([P, S], F32, name="gap%d" % t)
-                nc.vector.tensor_tensor(gap[:], g5[:], h[t][:], ALU.subtract)
-                rise = keep.tile([P, S], F32, name="rise%d" % t)
-                fall = keep.tile([P, S], F32, name="fall%d" % t)
-                nc.scalar.activation(rise[:], gap[:], ACT.Relu)
-                nc.scalar.activation(fall[:], rise[:], ACT.Copy, scale=-1.0)
-                nc.vector.tensor_tensor(page[:].indirect(n3_t[:]), h[t][:], rise[:], ALU.add)
-                nc.vector.tensor_tensor(page[:].indirect(n4_t[:]), g5[:], fall[:], ALU.add)
-            nc.sync.dma_start(out_rows[t], page[:])
+                nc.scalar.activation(g5[t][:, cols(c)], h[t][:].indirect(entries(n5_t, c)), ACT.Copy)
+
+        def lift(t):
+            gap = keep.tile([P, S], F32, name="gap", tag=gap_tag[t])
+            nc.gpsimd.tensor_tensor(gap[:], g5[t][:], h[t][:], ALU.subtract)
+            rise[t] = keep.tile([P, S], F32, name="rise", tag="rise%d" % t)
+            nc.scalar.activation(rise[t][:], gap[:], ACT.Relu)
+
+        def put_up(t):
+            fetch(t)
+            lift(t)
+            nc.gpsimd.tensor_tensor(up[t][:], h[t][:], rise[t][:], ALU.add)
+            nc.vector.tensor_copy(page[t][:].indirect(n3_t[:]), up[t][:])
+
+        def put_dn(t):
+            nc.gpsimd.tensor_tensor(dn[t][:], g5[t][:], rise[t][:], ALU.subtract)
+            nc.vector.tensor_copy(page[t][:].indirect(n4_t[:]), dn[t][:])
+            nc.sync.dma_start(out_rows[t], page[t][:])
+
+        fetch(0)
+        for c in range(2):
+            nc.vector.tensor_tensor(up[0][:, cols(c)], h[0][:, cols(c)], g5[0][:, cols(c)], ALU.max)
+            nc.vector.tensor_copy(page[0][:].indirect(entries(n3_t, c)), up[0][:, cols(c)])
+        nc.vector.tensor_tensor(dn[0][:], h[0][:], g5[0][:], ALU.min)
+        nc.vector.tensor_copy(page[0][:].indirect(n4_t[:]), dn[0][:])
+        nc.sync.dma_start(out_rows[0], page[0][:])
+        put_up(1)
+        put_up(2)
+        put_dn(1)
+        put_up(3)
+        put_dn(2)
+        put_dn(3)

@@ -47,40 +47,35 @@ def tile_picked_hdenseunderpagmx_none_p_kernel(
 
         ws_raw = keep.tile([P, S], U8, name="ws_raw", align_bytes=64)
         nc.sync.dma_start(ws_raw[:].bitcast(I32), spread(w1_scales))
+        offs_t = load_list("offs_t", offs)
         xs_win = keep.tile([P, TABLE], U8, name="xs_win", align_bytes=64)
         nc.sync.dma_start(xs_win[:].bitcast(I32), spread(x_scales))
-        offs_t = load_list("offs_t", offs)
+        w_raw = keep.tile([P, 2 * S], U8, name="w_raw", align_bytes=64)
+        nc.sync.dma_start(w_raw[:].bitcast(I32), w1_words[0].bitcast(I32))
         k1_t = load_list("k1_t", k1)
         n1_t = load_list("n1_t", n1)
+        n2_t = load_list("n2_t", n2)
         xw_win = keep.tile([P, TABLE], I32, name="xw_win", tag="table", align_bytes=64)
         nc.sync.dma_start(xw_win[:], x_words[0].rearrange("p n t -> p (n t)").bitcast(I32))
-        n2_t = load_list("n2_t", n2)
         n5_t = load_list("n5_t", n5)
         n3_t = load_list("n3_t", n3)
         n4_t = load_list("n4_t", n4)
 
-        w_raw = keep.tile([P, 2 * S], U8, name="w_raw", align_bytes=64)
-        nc.gpsimd.dma_start(w_raw[:].bitcast(I32), w1_words[0].bitcast(I32))
         ds_win = keep.tile([P, TABLE], U8, name="ds_win", align_bytes=64)
         nc.vector.memset(ds_win[:].bitcast(I32), 0)
-        nc.gpsimd.dma_start(ds_win[0:P:8, :].bitcast(I32), d_scales[0].bitcast(I32))
+        nc.sync.dma_start(ds_win[0:P:8, :].bitcast(I32), d_scales[0].bitcast(I32))
         gs_t = keep.tile([P, PACK], F32, name="gs_t")
         nc.gpsimd.dma_start(gs_t[:], gs.rearrange("(p t) o -> p (t o)", t=PACK))
 
         planes = keep.tile([P, 2 * S], U8, name="planes", align_bytes=64)
         xs = planes[:, 0:S]
         ws = planes[:, S : 2 * S]
-        staged = keep.tile([P, 2 * S], U8, name="staged", align_bytes=64)
         xs_got = keep.tile([P, S], U8, name="xs_got", align_bytes=64)
-        nc.vector.tensor_copy(
-            staged[:, S : 2 * S].rearrange("p (t m) -> p t m", t=PACK), ws_raw[:].rearrange("p (m t) -> p t m", t=PACK)
-        )
+        nc.vector.tensor_copy(ws.rearrange("p (t m) -> p t m", t=PACK), ws_raw[:].rearrange("p (m t) -> p t m", t=PACK))
         nc.vector.tensor_copy(xs_got[:], xs_win[:].indirect(offs_t[:]))
-        nc.vector.tensor_copy(ws.bitcast(I32), staged[:, S : 2 * S].bitcast(I32))
-        nc.vector.tensor_copy(staged[:, 0:S].bitcast(I32), xs_got[:].bitcast(I32))
         nc.vector.tensor_copy(xs.bitcast(I32), xs_got[:].bitcast(I32))
         for r in range(1, 4):
-            nc.scalar.dma_start(planes[r:P:32, :].bitcast(I32), staged[8 * r : P : 32, :].bitcast(I32))
+            nc.sync.dma_start(planes[r:P:32, :].bitcast(I32), planes[8 * r : P : 32, :].bitcast(I32))
 
         w = keep.tile([P, 2 * S], U8, name="w", align_bytes=64)
         nc.scalar.copy(
@@ -90,7 +85,7 @@ def tile_picked_hdenseunderpagmx_none_p_kernel(
 
         xw = keep.tile([P, S], U32, name="xw", align_bytes=64)
         y = [keep.tile([P, S], F32, name="y%d" % t) for t in range(PACK)]
-        y_ps = [[psum.tile([P, 2, HALF], F32, name="y_ps%d%d" % (c, a)) for a in range(2)] for c in range(2)]
+        y_ps = [[psum.tile([P, 2, HALF], F32, name="y_ps", tag="y_ps%d%d" % (c, a)) for a in range(2)] for c in range(2)]
         for c in range(2):
             nc.vector.tensor_copy(xw[:, cols(c)], xw_win[:].bitcast(U32).indirect(entries(offs_t, c)))
         dw_win = keep.tile([P, TABLE], I32, name="dw_win", tag="table", align_bytes=64)
@@ -98,12 +93,6 @@ def tile_picked_hdenseunderpagmx_none_p_kernel(
 
         ds_got = keep.tile([P, S], U8, name="ds_got", align_bytes=64)
         nc.vector.tensor_copy(ds_got[:], ds_win[:].indirect(k1_t[:]))
-        ds = keep.tile([P, S], U8, name="ds", align_bytes=64)
-        nc.vector.tensor_copy(
-            ds[:].rearrange("p (t m) -> p t m", t=PACK), ds_got[:].rearrange("p (m t) -> p t m", t=PACK)
-        )
-        for r in range(1, 4):
-            nc.sync.dma_start(ds[r:P:32, :].bitcast(I32), ds[8 * r : P : 32, :].bitcast(I32))
 
         for a in range(2):
             for c in range(2):
@@ -123,36 +112,42 @@ def tile_picked_hdenseunderpagmx_none_p_kernel(
                     else:
                         nc.vector.tensor_copy(y[t][:, cols(c)], y_ps[c][a][:, t % 2, :])
 
+        ds = keep.tile([P, S], U8, name="ds", align_bytes=64)
+        nc.vector.tensor_copy(
+            ds[:].rearrange("p (t m) -> p t m", t=PACK), ds_got[:].rearrange("p (m t) -> p t m", t=PACK)
+        )
+        for r in range(1, 4):
+            nc.sync.dma_start(ds[r:P:32, :].bitcast(I32), ds[8 * r : P : 32, :].bitcast(I32))
+
         zw = keep.tile([P, S], U32, name="zw", align_bytes=64)
         zs = keep.tile([P, S], U8, name="zs", align_bytes=64)
         dw_got = keep.tile([P, S], U32, name="dw_got", align_bytes=64)
         dw = keep.tile([P, S], U32, name="dw", align_bytes=64)
-        h_ps = [[psum.tile([P, 2, HALF], F32, name="h_ps%d%d" % (c, a)) for a in range(2)] for c in range(2)]
+        h_ps = {}
         h = [keep.tile([P, S], F32, name="h", tag="h%d" % t) for t in range(PACK)]
         for c in range(2):
-            zp = keep.tile([P, PACK, HALF], BF16, name="zp%d" % c, align_bytes=64)
+            diff = keep.tile([P, PACK, HALF], F32, name="diff%d" % c)
             for a in range(2):
                 g1 = keep.tile([P, 2, HALF], F32, name="g1_%d%d" % (c, a))
                 g2 = keep.tile([P, 2, HALF], F32, name="g2_%d%d" % (c, a))
                 low = keep.tile([P, 2, HALF], F32, name="low%d%d" % (c, a))
-                diff = keep.tile([P, 2, HALF], F32, name="diff%d%d" % (c, a))
                 for j in range(2):
                     t = 2 * a + j
                     nc.scalar.activation(g1[:, j, :], y[t][:].indirect(entries(n1_t, c)), ACT.Copy)
-                    if c == 0 and a == 0:
+                    if c == 0 and t < 3:
                         nc.vector.tensor_copy(g2[:, j, :], y[t][:].indirect(entries(n2_t, c)))
                     else:
                         nc.scalar.activation(g2[:, j, :], y[t][:].indirect(entries(n2_t, c)), ACT.Copy)
                 spans = [slice(0, 1), slice(1, 2)] if (c, a) == (1, 1) else [slice(0, 2)]
                 for span in spans:
                     nc.vector.tensor_tensor(low[:, span, :], g1[:, span, :], g2[:, span, :], ALU.min)
-                    nc.vector.tensor_tensor(diff[:, span, :], y_ps[c][a][:, span, :], low[:, span, :], ALU.subtract)
-                    for j in range(span.start, span.stop):
-                        t = 2 * a + j
-                        nc.vector.tensor_scalar(zp[:, t, :], diff[:, j, :], gs_t[:, t : t + 1], None, ALU.mult)
+                    nc.vector.tensor_tensor(diff[:, 2 * a + span.start : 2 * a + span.stop, :], y_ps[c][a][:, span, :], low[:, span, :], ALU.subtract)
             zi = keep.tile([P, HALF, PACK], BF16, name="zi%d" % c, align_bytes=64)
-            nc.vector.tensor_copy(
-                zi[:].rearrange("p (a i) t -> p a t i", i=4), zp[:].rearrange("p t (a i) -> p a t i", i=4)
+            nc.vector.tensor_tensor(
+                zi[:].rearrange("p (a i) t -> p a t i", i=4),
+                diff[:].rearrange("p t (a i) -> p a t i", i=4),
+                gs_t[:].unsqueeze(1).unsqueeze(3).to_broadcast([P, HALF // 4, PACK, 4]),
+                ALU.mult,
             )
             nc.vector.quantize_mx(
                 out=zw[:, cols(c)].bitcast(FP8X4), scales=zs[:, cols(c)], in_=zi[:].rearrange("p n t -> p (n t)")
@@ -162,9 +157,17 @@ def tile_picked_hdenseunderpagmx_none_p_kernel(
                 nc.vector.tensor_copy(
                     dw[:].rearrange("p (t m) -> p m t", t=PACK), dw_got[:].rearrange("p (m t) -> p m t", t=PACK)
                 )
+            if c == 0:
+                pairs = [psum.tile([P, 2, HALF], F32, name="h_ps0%d" % a) for a in range(2)]
             for t in range(PACK):
+                if c == 0:
+                    h_ps[t, c] = pairs[t // 2][:, t % 2, :]
+                else:
+                    tag = ["h_ps10", "h_ps11", "y_ps00", "y_ps01"][t]
+                    bank = psum.tile([P, HALF], F32, name="bank", tag=tag)
+                    h_ps[t, c] = bank[:]
                 nc.tensor.matmul_mx(
-                    out=h_ps[c][t // 2][:, t % 2, :],
+                    out=h_ps[t, c],
                     lhsT=dw[:, P * t : P * (t + 1)].bitcast(FP8X4),
                     lhsT_scale=ds[:, P * t : P * (t + 1)],
                     rhs=zw[:, cols(c)].bitcast(FP8X4),
@@ -174,51 +177,32 @@ def tile_picked_hdenseunderpagmx_none_p_kernel(
                 )
 
         out_rows = out.rearrange("(p t) w -> t p w", t=PACK)
-        g5 = {}
-        rise = {}
-        gap_tag = {1: "gap1", 2: "gap2", 3: "h1"}
-        g5_tag = ["g5_0", "g5_1", "g5_2", gap_tag[1]]
-        up = [keep.tile([P, S], F32, name="up%d" % t) for t in range(PACK)]
-        dn = [keep.tile([P, S], F32, name="dn%d" % t) for t in range(PACK)]
+        g5 = [keep.tile([P, S], F32, name="g5_%d" % t) for t in range(PACK)]
         page = [keep.tile([P, PAGE], F32, name="page%d" % t) for t in range(PACK)]
-
-        def fetch(t):
-            nc.scalar.activation(h[t][:, cols(0)], h_ps[0][t // 2][:, t % 2, :], ACT.Copy, scale=0.0625)
+        for t in range(PACK):
+            nc.scalar.activation(h[t][:, cols(0)], h_ps[t, 0], ACT.Copy, scale=0.0625)
             if t == 0:
-                nc.vector.tensor_scalar(h[t][:, cols(1)], h_ps[1][t // 2][:, t % 2, :], 0.0625, None, ALU.mult)
+                nc.vector.tensor_scalar(h[t][:, cols(1)], h_ps[t, 1], 0.0625, None, ALU.mult)
             else:
-                nc.scalar.activation(h[t][:, cols(1)], h_ps[1][t // 2][:, t % 2, :], ACT.Copy, scale=0.0625)
-            g5[t] = keep.tile([P, S], F32, name="g5", tag=g5_tag[t])
+                nc.scalar.activation(h[t][:, cols(1)], h_ps[t, 1], ACT.Copy, scale=0.0625)
             for c in range(2):
                 nc.scalar.activation(g5[t][:, cols(c)], h[t][:].indirect(entries(n5_t, c)), ACT.Copy)
-
-        def lift(t):
-            gap = keep.tile([P, S], F32, name="gap", tag=gap_tag[t])
-            nc.gpsimd.tensor_tensor(gap[:], g5[t][:], h[t][:], ALU.subtract)
-            rise[t] = keep.tile([P, S], F32, name="rise", tag="rise%d" % t)
-            nc.scalar.activation(rise[t][:], gap[:], ACT.Relu)
-
-        def put_up(t):
-            fetch(t)
-            lift(t)
-            nc.gpsimd.tensor_tensor(up[t][:], h[t][:], rise[t][:], ALU.add)
-            nc.vector.tensor_copy(page[t][:].indirect(n3_t[:]), up[t][:])
-
-        def put_dn(t):
-            nc.gpsimd.tensor_tensor(dn[t][:], g5[t][:], rise[t][:], ALU.subtract)
-            nc.vector.tensor_copy(page[t][:].indirect(n4_t[:]), dn[t][:])
+            if t == 0:
+                up = keep.tile([P, S], F32, name="up")
+                dn = keep.tile([P, S], F32, name="dn")
+                for c in range(2):
+                    nc.vector.tensor_tensor(up[:, cols(c)], h[t][:, cols(c)], g5[t][:, cols(c)], ALU.max)
+                    if c == 1:
+                        nc.vector.tensor_tensor(dn[:], h[t][:], g5[t][:], ALU.min)
+                    nc.vector.tensor_copy(page[t][:].indirect(entries(n3_t, c)), up[:, cols(c)])
+                nc.vector.tensor_copy(page[t][:].indirect(n4_t[:]), dn[:])
+            else:
+                gap = keep.tile([P, S], F32, name="gap%d" % t)
+                nc.gpsimd.tensor_tensor(gap[:], g5[t][:], h[t][:], ALU.subtract)
+                rise = keep.tile([P, S], F32, name="rise%d" % t)
+                fall = keep.tile([P, S], F32, name="fall%d" % t)
+                nc.scalar.activation(rise[:], gap[:], ACT.Relu)
+                nc.scalar.activation(fall[:], rise[:], ACT.Copy, scale=-1.0)
+                nc.vector.tensor_tensor(page[t][:].indirect(n3_t[:]), h[t][:], rise[:], ALU.add)
+                nc.vector.tensor_tensor(page[t][:].indirect(n4_t[:]), g5[t][:], fall[:], ALU.add)
             nc.sync.dma_start(out_rows[t], page[t][:])
-
-        fetch(0)
-        for c in range(2):
-            nc.vector.tensor_tensor(up[0][:, cols(c)], h[0][:, cols(c)], g5[0][:, cols(c)], ALU.max)
-            nc.vector.tensor_copy(page[0][:].indirect(entries(n3_t, c)), up[0][:, cols(c)])
-        nc.vector.tensor_tensor(dn[0][:], h[0][:], g5[0][:], ALU.min)
-        nc.vector.tensor_copy(page[0][:].indirect(n4_t[:]), dn[0][:])
-        nc.sync.dma_start(out_rows[0], page[0][:])
-        put_up(1)
-        put_up(2)
-        put_dn(1)
-        put_up(3)
-        put_dn(2)
-        put_dn(3)

from contextlib import ExitStack

import concourse.mybir as mybir

F32 = mybir.dt.float32
BF16 = mybir.dt.bfloat16
I32 = mybir.dt.int32
U32 = mybir.dt.uint32
U16 = mybir.dt.uint16
U8 = mybir.dt.uint8
FP8X4 = mybir.dt.float8_e4m3fn_x4
FP4X4 = mybir.dt.float4_e2m1fn_x4
ALU = mybir.AluOpType
ACT = mybir.ActivationFunctionType

P = 128
PACK = 4
TABLE = 2048
S = 512
PAGE = 1024
HALF = 256
FLOPS = 2 * 2 * 512 * 512 * 512


def tile_picked_hdenseunderpagmx_none_p_kernel(
    tc, x_words, x_scales, w1_words, w1_scales, gs, d_words, d_scales, offs, n1, n2, k1, n3, n4, n5, out
):
    nc = tc.nc
    with ExitStack() as ctx:
        keep = ctx.enter_context(tc.tile_pool(name="keep", bufs=1))
        psum = ctx.enter_context(tc.psum_pool(name="psum", bufs=1))

        def load_list(name, src):
            tile = keep.tile([P, S // 16], U16, name=name)
            nc.sync.dma_start(tile[:], src)
            return tile

        def entries(lst, c):
            return lst[:, c * HALF // 16 : (c + 1) * HALF // 16]

        def cols(c):
            return slice(c * HALF, (c + 1) * HALF)

        def spread(scales):
            rows = scales[0].bitcast(I32)
            return rows.unsqueeze(1).to_broadcast([16, 8, rows.shape[1]])

        ws_raw = keep.tile([P, S], U8, name="ws_raw", align_bytes=64)
        nc.sync.dma_start(ws_raw[:].bitcast(I32), spread(w1_scales))
        offs_t = load_list("offs_t", offs)
        xs_win = keep.tile([P, TABLE], U8, name="xs_win", align_bytes=64)
        nc.sync.dma_start(xs_win[:].bitcast(I32), spread(x_scales))
        w_raw = keep.tile([P, 2 * S], U8, name="w_raw", align_bytes=64)
        nc.sync.dma_start(w_raw[:].bitcast(I32), w1_words[0].bitcast(I32))
        k1_t = load_list("k1_t", k1)
        n1_t = load_list("n1_t", n1)
        n2_t = load_list("n2_t", n2)
        xw_win = keep.tile([P, TABLE], I32, name="xw_win", tag="table", align_bytes=64)
        nc.sync.dma_start(xw_win[:], x_words[0].rearrange("p n t -> p (n t)").bitcast(I32))
        n5_t = load_list("n5_t", n5)
        n3_t = load_list("n3_t", n3)
        n4_t = load_list("n4_t", n4)

        ds_win = keep.tile([P, TABLE], U8, name="ds_win", align_bytes=64)
        nc.vector.memset(ds_win[:].bitcast(I32), 0)
        nc.sync.dma_start(ds_win[0:P:8, :].bitcast(I32), d_scales[0].bitcast(I32))
        gs_t = keep.tile([P, PACK], F32, name="gs_t")
        nc.gpsimd.dma_start(gs_t[:], gs.rearrange("(p t) o -> p (t o)", t=PACK))

        planes = keep.tile([P, 2 * S], U8, name="planes", align_bytes=64)
        xs = planes[:, 0:S]
        ws = planes[:, S : 2 * S]
        xs_got = keep.tile([P, S], U8, name="xs_got", align_bytes=64)
        nc.vector.tensor_copy(ws.rearrange("p (t m) -> p t m", t=PACK), ws_raw[:].rearrange("p (m t) -> p t m", t=PACK))
        nc.vector.tensor_copy(xs_got[:], xs_win[:].indirect(offs_t[:]))
        nc.vector.tensor_copy(xs.bitcast(I32), xs_got[:].bitcast(I32))
        for r in range(1, 4):
            nc.sync.dma_start(planes[r:P:32, :].bitcast(I32), planes[8 * r : P : 32, :].bitcast(I32))

        w = keep.tile([P, 2 * S], U8, name="w", align_bytes=64)
        nc.scalar.copy(
            w[:].bitcast(U16).rearrange("p (t m) -> p t m", t=PACK),
            w_raw[:].bitcast(U16).rearrange("p (m t) -> p t m", t=PACK),
        )

        xw = keep.tile([P, S], U32, name="xw", align_bytes=64)
        y = [keep.tile([P, S], F32, name="y%d" % t) for t in range(PACK)]
        y_ps = [[psum.tile([P, 2, HALF], F32, name="y_ps", tag="y_ps%d%d" % (c, a)) for a in range(2)] for c in range(2)]
        for c in range(2):
            nc.vector.tensor_copy(xw[:, cols(c)], xw_win[:].bitcast(U32).indirect(entries(offs_t, c)))
        dw_win = keep.tile([P, TABLE], I32, name="dw_win", tag="table", align_bytes=64)
        nc.sync.dma_start(dw_win[:], d_words[0].rearrange("p n t -> p (n t)").bitcast(I32))

        ds_got = keep.tile([P, S], U8, name="ds_got", align_bytes=64)
        nc.vector.tensor_copy(ds_got[:], ds_win[:].indirect(k1_t[:]))

        for a in range(2):
            for c in range(2):
                for t in (2 * a, 2 * a + 1):
                    nc.tensor.matmul_mx(
                        out=y_ps[c][a][:, t % 2, :],
                        lhsT=w[:, 2 * P * t : 2 * P * (t + 1)].bitcast(FP4X4),
                        lhsT_scale=ws[:, P * t : P * (t + 1)],
                        rhs=xw[:, cols(c)].bitcast(FP8X4),
                        rhs_scale=xs[:, cols(c)],
                        start=True,
                        stop=True,
                    )
                for t in (2 * a, 2 * a + 1):
                    if c == 0:
                        nc.scalar.copy(y[t][:, cols(c)], y_ps[c][a][:, t % 2, :])
                    else:
                        nc.vector.tensor_copy(y[t][:, cols(c)], y_ps[c][a][:, t % 2, :])

        ds = keep.tile([P, S], U8, name="ds", align_bytes=64)
        nc.vector.tensor_copy(
            ds[:].rearrange("p (t m) -> p t m", t=PACK), ds_got[:].rearrange("p (m t) -> p t m", t=PACK)
        )
        for r in range(1, 4):
            nc.sync.dma_start(ds[r:P:32, :].bitcast(I32), ds[8 * r : P : 32, :].bitcast(I32))

        zw = keep.tile([P, S], U32, name="zw", align_bytes=64)
        zs = keep.tile([P, S], U8, name="zs", align_bytes=64)
        dw_got = keep.tile([P, S], U32, name="dw_got", align_bytes=64)
        dw = keep.tile([P, S], U32, name="dw", align_bytes=64)
        h_ps = {}
        h = [keep.tile([P, S], F32, name="h", tag="h%d" % t) for t in range(PACK)]
        for c in range(2):
            diff = keep.tile([P, PACK, HALF], F32, name="diff%d" % c)
            for a in range(2):
                g1 = keep.tile([P, 2, HALF], F32, name="g1_%d%d" % (c, a))
                g2 = keep.tile([P, 2, HALF], F32, name="g2_%d%d" % (c, a))
                low = keep.tile([P, 2, HALF], F32, name="low%d%d" % (c, a))
                for j in range(2):
                    t = 2 * a + j
                    nc.scalar.activation(g1[:, j, :], y[t][:].indirect(entries(n1_t, c)), ACT.Copy)
                    if c == 0 and t < 3:
                        nc.vector.tensor_copy(g2[:, j, :], y[t][:].indirect(entries(n2_t, c)))
                    else:
                        nc.scalar.activation(g2[:, j, :], y[t][:].indirect(entries(n2_t, c)), ACT.Copy)
                spans = [slice(0, 1), slice(1, 2)] if (c, a) == (1, 1) else [slice(0, 2)]
                for span in spans:
                    nc.vector.tensor_tensor(low[:, span, :], g1[:, span, :], g2[:, span, :], ALU.min)
                    nc.vector.tensor_tensor(diff[:, 2 * a + span.start : 2 * a + span.stop, :], y_ps[c][a][:, span, :], low[:, span, :], ALU.subtract)
            zi = keep.tile([P, HALF, PACK], BF16, name="zi%d" % c, align_bytes=64)
            nc.vector.tensor_tensor(
                zi[:].rearrange("p (a i) t -> p a t i", i=4),
                diff[:].rearrange("p t (a i) -> p a t i", i=4),
                gs_t[:].unsqueeze(1).unsqueeze(3).to_broadcast([P, HALF // 4, PACK, 4]),
                ALU.mult,
            )
            nc.vector.quantize_mx(
                out=zw[:, cols(c)].bitcast(FP8X4), scales=zs[:, cols(c)], in_=zi[:].rearrange("p n t -> p (n t)")
            )
            if c == 0:
                nc.vector.tensor_copy(dw_got[:], dw_win[:].bitcast(U32).indirect(k1_t[:]))
                nc.vector.tensor_copy(
                    dw[:].rearrange("p (t m) -> p m t", t=PACK), dw_got[:].rearrange("p (m t) -> p m t", t=PACK)
                )
            if c == 0:
                pairs = [psum.tile([P, 2, HALF], F32, name="h_ps0%d" % a) for a in range(2)]
            for t in range(PACK):
                if c == 0:
                    h_ps[t, c] = pairs[t // 2][:, t % 2, :]
                else:
                    tag = ["h_ps10", "h_ps11", "y_ps00", "y_ps01"][t]
                    bank = psum.tile([P, HALF], F32, name="bank", tag=tag)
                    h_ps[t, c] = bank[:]
                nc.tensor.matmul_mx(
                    out=h_ps[t, c],
                    lhsT=dw[:, P * t : P * (t + 1)].bitcast(FP8X4),
                    lhsT_scale=ds[:, P * t : P * (t + 1)],
                    rhs=zw[:, cols(c)].bitcast(FP8X4),
                    rhs_scale=zs[:, cols(c)],
                    start=True,
                    stop=True,
                )

        out_rows = out.rearrange("(p t) w -> t p w", t=PACK)
        g5 = [keep.tile([P, S], F32, name="g5_%d" % t) for t in range(PACK)]
        page = [keep.tile([P, PAGE], F32, name="page%d" % t) for t in range(PACK)]
        for t in range(PACK):
            nc.scalar.activation(h[t][:, cols(0)], h_ps[t, 0], ACT.Copy, scale=0.0625)
            if t == 0:
                nc.vector.tensor_scalar(h[t][:, cols(1)], h_ps[t, 1], 0.0625, None, ALU.mult)
            else:
                nc.scalar.activation(h[t][:, cols(1)], h_ps[t, 1], ACT.Copy, scale=0.0625)
            for c in range(2):
                nc.scalar.activation(g5[t][:, cols(c)], h[t][:].indirect(entries(n5_t, c)), ACT.Copy)
            if t == 0:
                up = keep.tile([P, S], F32, name="up")
                dn = keep.tile([P, S], F32, name="dn")
                for c in range(2):
                    nc.vector.tensor_tensor(up[:, cols(c)], h[t][:, cols(c)], g5[t][:, cols(c)], ALU.max)
                    if c == 1:
                        nc.vector.tensor_tensor(dn[:], h[t][:], g5[t][:], ALU.min)
                    nc.vector.tensor_copy(page[t][:].indirect(entries(n3_t, c)), up[:, cols(c)])
                nc.vector.tensor_copy(page[t][:].indirect(n4_t[:]), dn[:])
            else:
                gap = keep.tile([P, S], F32, name="gap%d" % t)
                nc.gpsimd.tensor_tensor(gap[:], g5[t][:], h[t][:], ALU.subtract)
                rise = keep.tile([P, S], F32, name="rise%d" % t)
                fall = keep.tile([P, S], F32, name="fall%d" % t)
                nc.scalar.activation(rise[:], gap[:], ACT.Relu)
                nc.scalar.activation(fall[:], rise[:], ACT.Copy, scale=-1.0)
                nc.vector.tensor_tensor(page[t][:].indirect(n3_t[:]), h[t][:], rise[:], ALU.add)
                nc.vector.tensor_tensor(page[t][:].indirect(n4_t[:]), g5[t][:], fall[:], ALU.add)
            nc.sync.dma_start(out_rows[t], page[t][:])
